import numpy as np
import ml_dtypes


def mxq(x, axis, fmt="e4m3"):
    dtype, down = {"e4m3": (ml_dtypes.float8_e4m3fn, 7), "e5m2": (ml_dtypes.float8_e5m2, 14)}[fmt]
    v = np.moveaxis(np.asarray(x, np.float32).astype(ml_dtypes.bfloat16).astype(np.float64), axis, -1)
    blocks = v.reshape(v.shape[:-1] + (-1, 32))
    amax = np.abs(blocks).max(-1, keepdims=True)
    byte = np.maximum(np.where(amax > 0, np.frexp(amax)[1] - 1 + 127, 0) - down, 1)
    scale = np.exp2(byte - 127.0)
    codes = (blocks / scale).astype(np.float32).astype(dtype).astype(np.float64)
    return np.moveaxis((codes * scale).reshape(v.shape), -1, axis)


WIDE = False


def mx_kscale(k):
    if not WIDE:
        return np.ones(k)
    levels = np.array([10, -10, 5, -5, 0])
    if k % 512:
        return np.exp2(np.random.permutation(np.resize(levels, k // 32))).repeat(32)
    a = np.empty((k // 512, 16))
    for p in range(k // 512):
        a[p, :8] = np.random.permutation(np.resize(levels, 8))
        for g in range(8):
            far = levels[np.abs(levels - a[p, g]) >= 10]
            a[p, g + 8] = far[np.random.randint(len(far))]
    return np.exp2(a.ravel()).repeat(32)


BF16 = ml_dtypes.bfloat16


def bf(x):
    return np.asarray(x, np.float32).astype(BF16)


def f64(x):
    return np.asarray(x).astype(np.float64)


E2M1 = np.array([0.0, 0.5, 1.0, 1.5, 2.0, 3.0, 4.0, 6.0, -0.0, -0.5, -1.0, -1.5, -2.0, -3.0, -4.0, -6.0])


def pack_weight(w, fmt):
    k, n = w.shape
    w = f64(bf(w)).reshape(k // 32, 32, n)
    amax = np.abs(w).max(1)
    if fmt == "e4m3":
        byte = np.frexp(amax)[1] - 1 + 127 - 7
    else:
        mant, ex = np.frexp(amax / 6.0)
        byte = np.where(mant > 0.5, ex, ex - 1) + 127
    byte = np.clip(np.where(amax > 0, byte, 1), 1, 254)
    scaled = (w * np.exp2(127.0 - byte)[:, None, :]).reshape(k, n).astype(np.float32)
    by_word = np.ascontiguousarray(scaled.reshape(k // 512, 128, 4, n).transpose(0, 1, 3, 2))
    if fmt == "e4m3":
        words = by_word.astype(ml_dtypes.float8_e4m3fn).view(np.uint8)
    else:
        c = by_word.astype(ml_dtypes.float4_e2m1fn).view(np.uint8) & 0xF
        words = c[..., 0::2] | (c[..., 1::2] << 4)
    return np.ascontiguousarray(words), np.ascontiguousarray(byte.astype(np.uint8).reshape(k // 512, 16, n))


def unpack_weight(words, scales, fmt):
    g, p, n, _ = words.shape
    if fmt == "e4m3":
        vals = np.ascontiguousarray(words).view(ml_dtypes.float8_e4m3fn).astype(np.float64)
    else:
        nib = np.empty((g, p, n, 4), np.uint8)
        nib[..., 0::2] = words & 0xF
        nib[..., 1::2] = words >> 4
        vals = E2M1[nib]
    vals = vals * np.repeat(np.exp2(scales.astype(np.float64) - 127.0), 8, axis=1)[..., None]
    return vals.transpose(0, 1, 3, 2).reshape(g * 512, n)
def pack4(w):
    words, scales = pack_weight(w, "e2m1")
    return words.reshape(words.shape[0], 128, -1), scales


def unpack4(words, scales):
    return unpack_weight(words.reshape(words.shape[0], 128, -1, 2), scales, "e2m1")


def planes(Y):
    n, m = Y.shape
    b = f64(bf(Y)).reshape(n // 32, 32, m)
    amax = np.abs(b).max(1)
    byte = np.clip(np.where(amax > 0, np.frexp(amax)[1] - 1 + 127 - 7, 1), 1, 254)
    codes = (b * np.exp2(127.0 - byte)[:, None, :]).reshape(n, m).astype(np.float32).astype(ml_dtypes.float8_e4m3fn).view(np.uint8)
    words = codes.reshape(n // 512, 128, 4, m).transpose(0, 1, 3, 2)
    return np.ascontiguousarray(words), np.ascontiguousarray(byte.astype(np.uint8).reshape(n // 512, 16, m))


N, B, R, T = 1024, 512, 1024, 1024


def setup_inputs():
    s, t, v = mx_kscale(B), mx_kscale(R), mx_kscale(B)
    ib, ir = 1.0 / np.sqrt(B), 1.0 / np.sqrt(R)
    delta = bf(np.random.uniform(-1.0, 1.0, (N, B)) * ib * s[None, :])
    rd = bf(1.0 + 0.1 * np.random.standard_normal(B))
    u = bf(np.random.standard_normal((B, R)) * ir / s[:, None] * t[None, :])
    wr = bf(np.random.standard_normal((N, R)) * ir * t[None, :])
    q_words, q_scales = pack4((np.random.standard_normal((N, B)) * ib / v[None, :]).T)
    return {
        "delta": delta,
        "rd": rd,
        "u": u,
        "wr": wr,
        "q_words": q_words,
        "q_scales": q_scales,
        "xb": bf(np.random.standard_normal((T, B)) * v[None, :]),
        "xr": bf(np.random.standard_normal((T, R)) / t[None, :]),
    }


def compensate(delta, rd, u, wr):
    e = delta * rd[None, :]
    c = mxq(e, 1, "e4m3") @ mxq(u, 0, "e4m3")
    return wr - c


def core(delta, rd, u, wr, q_words, q_scales, xb, xr):
    wn = compensate(f64(delta), f64(rd), f64(u), f64(wr))
    yr = mxq(f64(xr), 1, "e4m3") @ mxq(wn, 1, "e4m3").T
    yb = mxq(f64(xb), 1, "e4m3") @ unpack4(q_words, q_scales)
    y = yr + yb
    return y


def reference(delta, rd, u, wr, q_words, q_scales, xb, xr):
    R_out = core(delta, rd, u, wr, q_words, q_scales, xb, xr)
    words, scales = planes(R_out.T)
    return R_out, words, scales

@@ -1,0 +1,365 @@
+from contextlib import ExitStack
+
+import concourse.mybir as mybir
+from concourse.masks import make_identity
+
+N, B, R, T = 1024, 512, 1024, 1024
+FLOPS = 2 * (N * B * R + T * R * N + T * B * N)
+
+F32 = mybir.dt.float32
+BF16 = mybir.dt.bfloat16
+I32 = mybir.dt.int32
+U32 = mybir.dt.uint32
+U8 = mybir.dt.uint8
+FP8X4 = mybir.dt.float8_e4m3fn_x4
+FP4X4 = mybir.dt.float4_e2m1fn_x4
+SUB = mybir.AluOpType.subtract
+MULT = mybir.AluOpType.mult
+
+P = 128
+
+
+def tile_gptqlazyblockcompensatedoutput_x2_kernel(
+    tc, delta, rd, u, wr, q_words, q_scales, xb, xr, out_0, out_1, out_2
+):
+    nc = tc.nc
+    with ExitStack() as ctx:
+        keep = ctx.enter_context(tc.tile_pool(name="keep", bufs=1))
+        ring = ctx.enter_context(tc.tile_pool(name="ring", bufs=4))
+        tps = ctx.enter_context(tc.psum_pool(name="tps", bufs=3))
+        acc = ctx.enter_context(tc.psum_pool(name="acc", bufs=5))
+
+        def tl(shape, dt, nm):
+            t = keep.tile(shape, dt, name=nm, align_bytes=64)
+            return t
+
+        ident = tl([P, P], F32, "ident")
+        make_identity(nc, ident[:])
+        q_plane = tl([P, N], U8, "q_plane")
+        nc.gpsimd.memset(q_plane[:].bitcast(I32), 0)
+
+        rd4 = tl([P, 1, 2, 2], BF16, "rd4")
+        d_sb = [tl([P, 2, 2, B], BF16, "d_sb%d" % h) for h in range(2)]
+        u_sb = [tl([P, 4, 512], BF16, "u_sb%d" % h) for h in range(2)]
+        wr_sb = [tl([P, 2, R], BF16, "wr_sb%d" % i) for i in range(4)]
+        xr_sb = [tl([P, 2, R], BF16, "xr_sb%d" % i) for i in range(4)]
+        xb_sb = [tl([P, 2, 2, B], BF16, "xb_sb%d" % h) for h in range(2)]
+        q_w = tl([P, 2 * N], U8, "q_w")
+
+        def load_half(dst, src, h):
+            nc.sync.dma_start(
+                out=dst[:],
+                in_=src[h * 512 : (h + 1) * 512, :].rearrange("(b p a) k -> p b a k", p=P, a=2),
+            )
+
+        def load_block(dst, src, i):
+            nc.sync.dma_start(
+                out=dst[:], in_=src[i * 256 : (i + 1) * 256, :].rearrange("(p a) k -> p a k", a=2)
+            )
+
+        u_view = u.rearrange("(p j) r -> p j r", j=4)
+
+        nc.scalar.dma_start(
+            out=rd4[:].rearrange("p o u e -> p (o u e)"), in_=rd.rearrange("(p t) -> p t", t=4)
+        )
+        def load_u(g):
+            nc.sync.dma_start(out=u_sb[g][:], in_=u_view[:, :, g * 512 : (g + 1) * 512])
+
+        for h in range(2):
+            load_u(h)
+            load_half(d_sb[h], delta, h)
+        load_half(xb_sb[0], xb, 0)
+        for i in range(3):
+            load_block(wr_sb[i], wr, i)
+            load_block(xr_sb[i], xr, i)
+        nc.sync.dma_start(out=q_w[:].bitcast(I32), in_=q_words[0].bitcast(I32))
+        for q in range(4):
+            nc.sync.dma_start(
+                out=q_plane[32 * q : 32 * q + 4, :].bitcast(I32),
+                in_=q_scales[0, 4 * q : 4 * q + 4, :].bitcast(I32),
+            )
+        load_block(wr_sb[3], wr, 3)
+        load_block(xr_sb[3], xr, 3)
+        load_half(xb_sb[1], xb, 1)
+
+        eg = [tl([P, 512, 4], BF16, "eg%d" % h) for h in range(2)]
+        ug = [tl([P, 512, 4], BF16, "ug%d" % h) for h in range(2)]
+        wn = [tl([P, 2, 2, 2, P, 2], BF16, "wn%d" % i) for i in range(4)]
+        e_c = tl([P, N], U32, "e_c")
+        e_s = tl([P, N], U8, "e_s")
+        u_c = tl([P, R], U32, "u_c")
+        u_s = tl([P, R], U8, "u_s")
+        wn_c = [tl([P, N], U32, "wn_c%d" % g) for g in range(2)]
+        wn_s = [tl([P, N], U8, "wn_s%d" % g) for g in range(2)]
+        xr_c = [tl([P, 2, 256], U32, "xr_c%d" % i) for i in range(4)]
+        xr_s = [tl([P, 2, 256], U8, "xr_s%d" % i) for i in range(4)]
+        xb_c = tl([P, T], U32, "xb_c")
+        xb_s = tl([P, T], U8, "xb_s")
+
+        def quant(src, codes, scales):
+            nc.vector.quantize_mx(out=codes.bitcast(FP8X4), scales=scales, in_=src)
+
+        def transposes(words, offsets, step):
+            bank = tps.tile([P, 2, 2, P], F32, name="tp")
+            for uu in range(2):
+                for a in range(2):
+                    o = offsets[uu][a]
+                    nc.tensor.transpose(
+                        bank[:, uu, a, :], words[:, o : o + P * step - step + 1 : step], ident[:]
+                    )
+            return bank
+
+        def e_block(i):
+            h, b = i // 2, i % 2
+            words = d_sb[h][:].rearrange("p b a k -> p (b a k)").bitcast(F32)
+            bank = transposes(words, [[(b * 2 + a) * 256 + uu for a in range(2)] for uu in range(2)], 2)
+            nc.vector.tensor_tensor(
+                out=eg[h][:, b * 256 : (b + 1) * 256, :].rearrange("p c (u e) -> p c u e", u=2),
+                in0=bank[:].rearrange("p u a r -> p (u a r)").bitcast(BF16).rearrange("p (u c e) -> p c u e", u=2, e=2),
+                in1=rd4[:].to_broadcast([P, 256, 2, 2]),
+                op=MULT,
+            )
+
+        def e_quant(h):
+            s = slice(h * 512, (h + 1) * 512)
+            quant(eg[h][:].rearrange("p c t -> p (c t)"), e_c[:, s], e_s[:, s])
+
+        def u_copy(g, eng):
+            src = u_sb[g][:].rearrange("p j w -> p w j")
+            if eng == 0:
+                nc.vector.tensor_copy(out=ug[g][:], in_=src)
+            else:
+                nc.scalar.copy(out=ug[g][:], in_=src)
+
+        def u_quant(g):
+            s = slice(g * 512, (g + 1) * 512)
+            quant(ug[g][:].rearrange("p c t -> p (c t)"), u_c[:, s], u_s[:, s])
+
+        def stage1(i, a, g):
+            n0 = i * 256 + a * 128
+            bank = acc.tile([P, 512], F32, name="acc")
+            nc.tensor.matmul_mx(
+                out=bank[:],
+                lhsT=e_c[:, n0 : n0 + P].bitcast(FP8X4),
+                lhsT_scale=e_s[:, n0 : n0 + P],
+                rhs=u_c[:, g * 512 : (g + 1) * 512].bitcast(FP8X4),
+                rhs_scale=u_s[:, g * 512 : (g + 1) * 512],
+                start=True,
+                stop=True,
+            )
+            nc.vector.tensor_tensor(
+                out=wn[i][:, a, g, :, :, :],
+                in0=wr_sb[i][:, a, g * 512 : (g + 1) * 512].rearrange("p (k u e) -> p u k e", u=2, e=2),
+                in1=bank[:].rearrange("p (k u e) -> p u k e", u=2, e=2),
+                op=SUB,
+            )
+
+        wnt = {}
+
+        def wn_turn(i, g):
+            h = i // 2
+            if (h, g) not in wnt:
+                wnt_t = ring.tile([P, 512, 4], BF16, name="wnt", align_bytes=64)
+                wnt[(h, g)] = wnt_t
+            words = wn[i][:].rearrange("p a g u k e -> p (a g u k e)").bitcast(F32)
+            bank = transposes(words, [[((a * 2 + g) * 2 + uu) * P for a in range(2)] for uu in range(2)], 1)
+            b = i % 2
+            dst = wnt[(h, g)][:, b * 256 : (b + 1) * 256, :].rearrange("p c t -> p (c t)").bitcast(F32)
+            nc.scalar.copy(
+                out=dst.rearrange("p (r a u) -> p r a u", a=2, u=2),
+                in_=bank[:].rearrange("p u a r -> p r a u"),
+            )
+
+        def wn_quant(h, g):
+            s = slice(h * 512, (h + 1) * 512)
+            quant(wnt[(h, g)][:].rearrange("p c t -> p (c t)"), wn_c[g][:, s], wn_s[g][:, s])
+
+        xt = {}
+
+        def xr_turn(i):
+            xt_t = ring.tile([P, 2, 256, 4], BF16, name="xt", align_bytes=64)
+            xt[i] = xt_t
+            words = xr_sb[i][:].rearrange("p a k -> p (a k)").bitcast(F32)
+            for g in range(2):
+                bank = transposes(words, [[a * 512 + g * 256 + uu for a in range(2)] for uu in range(2)], 2)
+                dst = xt_t[:, g, :, :].rearrange("p c t -> p (c t)").bitcast(F32)
+                nc.scalar.copy(
+                    out=dst.rearrange("p (r a u) -> p r a u", a=2, u=2),
+                    in_=bank[:].rearrange("p u a r -> p r a u"),
+                )
+
+        def xr_quant(i):
+            quant(
+                xt[i][:].rearrange("p g c t -> p (g c t)"),
+                xr_c[i][:].rearrange("p g c -> p (g c)"),
+                xr_s[i][:].rearrange("p g c -> p (g c)"),
+            )
+
+        xbt = {}
+
+        def xb_turn(i):
+            h, b = i // 2, i % 2
+            if b == 0:
+                xbt_t = ring.tile([P, 512, 4], BF16, name="xbt", align_bytes=64)
+                xbt[h] = xbt_t
+            words = xb_sb[h][:].rearrange("p b a k -> p (b a k)").bitcast(F32)
+            bank = transposes(words, [[(b * 2 + a) * 256 + uu for a in range(2)] for uu in range(2)], 2)
+            dst = xbt[h][:, b * 256 : (b + 1) * 256, :].rearrange("p c t -> p (c t)").bitcast(F32)
+            nc.scalar.copy(
+                out=dst.rearrange("p (r a u) -> p r a u", a=2, u=2),
+                in_=bank[:].rearrange("p u a r -> p r a u"),
+            )
+
+        def xb_quant(h):
+            s = slice(h * 512, (h + 1) * 512)
+            quant(xbt[h][:].rearrange("p c t -> p (c t)"), xb_c[:, s], xb_s[:, s])
+
+        yo, yb, pc = {}, {}, {}
+        ps = [tl([P, T], U8, "ps%d" % h) for h in range(2)]
+
+        def y_mm(h, t):
+            tp = t // 2
+            if t % 2 == 0:
+                yo_t = ring.tile([P, 2, 512], F32, name="yo", align_bytes=64)
+                yb_t = ring.tile([P, 2, 2, P, 2], BF16, name="yb", align_bytes=64)
+                yo[(h, tp)] = yo_t
+                yb[(h, tp)] = yb_t
+            n = slice(h * 512, (h + 1) * 512)
+            bank = acc.tile([P, 512], F32, name="acc")
+            nc.tensor.matmul_mx(
+                out=bank[:],
+                lhsT=xb_c[:, t * P : (t + 1) * P].bitcast(FP8X4),
+                lhsT_scale=xb_s[:, t * P : (t + 1) * P],
+                rhs=q_w[:, h * 1024 : (h + 1) * 1024].bitcast(FP4X4),
+                rhs_scale=q_plane[:, n],
+                start=True,
+                stop=False,
+            )
+            c0 = (t % 2) * P
+            for g in range(2):
+                nc.tensor.matmul_mx(
+                    out=bank[:],
+                    lhsT=xr_c[tp][:, g, c0 : c0 + P].bitcast(FP8X4),
+                    lhsT_scale=xr_s[tp][:, g, c0 : c0 + P],
+                    rhs=wn_c[g][:, n].bitcast(FP8X4),
+                    rhs_scale=wn_s[g][:, n],
+                    start=False,
+                    stop=(g == 1),
+                )
+            nc.scalar.copy(out=yo[(h, tp)][:, t % 2, :], in_=bank[:])
+
+        def y_round(h, t):
+            tp = t // 2
+            n = slice(h * 512, (h + 1) * 512)
+            nc.vector.tensor_copy(
+                out=yb[(h, tp)][:, t % 2, :, :, :],
+                in_=yo[(h, tp)][:, t % 2, :].rearrange("p (k u e) -> p u k e", u=2, e=2),
+            )
+            if t % 2 == 1:
+                nc.sync.dma_start(
+                    out=out_0[tp * 256 : (tp + 1) * 256, n].rearrange("(t p) n -> p t n", p=P),
+                    in_=yo[(h, tp)][:],
+                )
+
+        yt = {}
+
+        def y_turn(h, tp):
+            words = yb[(h, tp)][:].rearrange("p t u k e -> p (t u k e)").bitcast(F32)
+            bank = transposes(words, [[(t * 2 + uu) * P for t in range(2)] for uu in range(2)], 1)
+            yt_t = ring.tile([P, 256, 4], BF16, name="yt", align_bytes=64)
+            yt[(h, tp)] = yt_t
+            nc.scalar.copy(
+                out=yt_t[:].rearrange("p c t -> p (c t)").bitcast(F32).rearrange("p (c u) -> p c u", u=2),
+                in_=bank[:].rearrange("p u t r -> p (t r) u"),
+            )
+
+        def y_quant(h, tp):
+            th = tp // 2
+            if tp % 2 == 0:
+                pc_t = ring.tile([P, 512], U32, name="pc", align_bytes=64)
+                pc[(h, th)] = pc_t
+            c = (tp % 2) * 256
+            quant(
+                yt[(h, tp)][:].rearrange("p c t -> p (c t)"),
+                pc[(h, th)][:, c : c + 256],
+                ps[h][:, tp * 256 : (tp + 1) * 256],
+            )
+            if tp % 2 == 1:
+                nc.sync.dma_start(
+                    out=out_1[h, :, th * 512 : (th + 1) * 512, :].rearrange("p m t -> p (m t)").bitcast(I32),
+                    in_=pc[(h, th)][:].bitcast(I32),
+                )
+            if tp == 3:
+                for q in range(4):
+                    nc.sync.dma_start(
+                        out=out_2[h, 4 * q : 4 * q + 4, :].bitcast(I32),
+                        in_=ps[h][32 * q : 32 * q + 4, :].bitcast(I32),
+                    )
+
+        def stage1_block(i):
+            for a in range(2):
+                for g in range(2):
+                    stage1(i, a, g)
+
+        def y_pair(h, tp):
+            y_mm(h, 2 * tp)
+            y_mm(h, 2 * tp + 1)
+
+        def y_round_pair(h, tp):
+            y_round(h, 2 * tp)
+            y_round(h, 2 * tp + 1)
+
+        with tc.manual_schedule():
+            u_copy(0, 0)
+            u_copy(1, 1)
+            e_block(0)
+            e_block(1)
+            u_quant(0)
+            e_quant(0)
+            e_block(2)
+            e_block(3)
+            u_quant(1)
+            xb_turn(0)
+            xb_turn(1)
+            stage1_block(0)
+            xr_turn(0)
+            e_quant(1)
+            xb_quant(0)
+            stage1_block(1)
+            xr_turn(1)
+            wn_turn(0, 0)
+            wn_turn(0, 1)
+            xr_quant(0)
+            stage1_block(2)
+            xr_turn(2)
+            wn_turn(1, 0)
+            wn_turn(1, 1)
+            xr_quant(1)
+            wn_quant(0, 0)
+            wn_quant(0, 1)
+            stage1_block(3)
+            xr_turn(3)
+            xb_turn(2)
+            xb_turn(3)
+            xr_quant(2)
+            y_pair(0, 0)
+            wn_turn(2, 0)
+            wn_turn(2, 1)
+            xr_quant(3)
+            xb_quant(1)
+            y_pair(0, 1)
+            y_round_pair(0, 0)
+            wn_turn(3, 0)
+            wn_turn(3, 1)
+            wn_quant(1, 0)
+            wn_quant(1, 1)
+            y_round_pair(0, 1)
+            pairs = [(h, tp) for h in range(2) for tp in range(4)]
+            for j in range(2, 8):
+                y_pair(*pairs[j])
+                y_turn(*pairs[j - 2])
+                y_round_pair(*pairs[j])
+                y_quant(*pairs[j - 2])
+            for j in range(6, 8):
+                y_turn(*pairs[j])
+                y_quant(*pairs[j])

@@ -33,10 +33,10 @@ def tile_gptqlazyblockcompensatedoutput_x2_kernel(
             t = keep.tile(shape, dt, name=nm, align_bytes=64)
             return t
 
-        ident = tl([P, P], F32, "ident")
-        make_identity(nc, ident[:])
         q_plane = tl([P, N], U8, "q_plane")
         nc.gpsimd.memset(q_plane[:].bitcast(I32), 0)
+        ident = tl([P, P], F32, "ident")
+        make_identity(nc, ident[:])
 
         rd4 = tl([P, 1, 2, 2], BF16, "rd4")
         d_sb = [tl([P, 2, 2, B], BF16, "d_sb%d" % h) for h in range(2)]
@@ -65,22 +65,34 @@ def tile_gptqlazyblockcompensatedoutput_x2_kernel(
         def load_u(g):
             nc.sync.dma_start(out=u_sb[g][:], in_=u_view[:, :, g * 512 : (g + 1) * 512])
 
-        for h in range(2):
-            load_u(h)
-            load_half(d_sb[h], delta, h)
-        load_half(xb_sb[0], xb, 0)
-        for i in range(3):
-            load_block(wr_sb[i], wr, i)
-            load_block(xr_sb[i], xr, i)
-        nc.sync.dma_start(out=q_w[:].bitcast(I32), in_=q_words[0].bitcast(I32))
-        for q in range(4):
+        def load_d(i):
+            h, b = i // 2, i % 2
             nc.sync.dma_start(
+                out=d_sb[h][:, b, :, :],
+                in_=delta[i * 256 : (i + 1) * 256, :].rearrange("(p a) k -> p a k", a=2),
+            )
+
+        for q in range(4):
+            nc.scalar.dma_start(
                 out=q_plane[32 * q : 32 * q + 4, :].bitcast(I32),
                 in_=q_scales[0, 4 * q : 4 * q + 4, :].bitcast(I32),
             )
-        load_block(wr_sb[3], wr, 3)
-        load_block(xr_sb[3], xr, 3)
+        load_d(0)
+        load_d(1)
+        load_block(xr_sb[0], xr, 0)
+        load_u(0)
+        load_half(d_sb[1], delta, 1)
+        load_half(xb_sb[0], xb, 0)
+        load_u(1)
+        load_block(wr_sb[0], wr, 0)
         load_half(xb_sb[1], xb, 1)
+        load_block(wr_sb[1], wr, 1)
+        load_block(xr_sb[1], xr, 1)
+        load_block(wr_sb[2], wr, 2)
+        load_block(xr_sb[2], xr, 2)
+        load_block(xr_sb[3], xr, 3)
+        nc.sync.dma_start(out=q_w[:].bitcast(I32), in_=q_words[0].bitcast(I32))
+        load_block(wr_sb[3], wr, 3)
 
         eg = [tl([P, 512, 4], BF16, "eg%d" % h) for h in range(2)]
         ug = [tl([P, 512, 4], BF16, "ug%d" % h) for h in range(2)]
@@ -120,16 +132,17 @@ def tile_gptqlazyblockcompensatedoutput_x2_kernel(
                 op=MULT,
             )
 
-        def e_quant(h):
-            s = slice(h * 512, (h + 1) * 512)
-            quant(eg[h][:].rearrange("p c t -> p (c t)"), e_c[:, s], e_s[:, s])
+        def e_quant(i):
+            h, b = i // 2, i % 2
+            s = slice(i * 256, (i + 1) * 256)
+            quant(eg[h][:, b * 256 : (b + 1) * 256, :].rearrange("p c t -> p (c t)"), e_c[:, s], e_s[:, s])
 
-        def u_copy(g, eng):
-            src = u_sb[g][:].rearrange("p j w -> p w j")
-            if eng == 0:
-                nc.vector.tensor_copy(out=ug[g][:], in_=src)
-            else:
-                nc.scalar.copy(out=ug[g][:], in_=src)
+        def u_copy(g, b, copy):
+            c = slice(b * 256, (b + 1) * 256)
+            copy(
+                out=ug[g][:, c, :].rearrange("p (c i) t -> p c t i", i=4),
+                in_=u_sb[g][:, :, c].rearrange("p t (c i) -> p c t i", i=4),
+            )
 
         def u_quant(g):
             s = slice(g * 512, (g + 1) * 512)
@@ -147,6 +160,9 @@ def tile_gptqlazyblockcompensatedoutput_x2_kernel(
                 start=True,
                 stop=True,
             )
+            return bank
+
+        def sub(i, a, g, bank):
             nc.vector.tensor_tensor(
                 out=wn[i][:, a, g, :, :, :],
                 in0=wr_sb[i][:, a, g * 512 : (g + 1) * 512].rearrange("p (k u e) -> p u k e", u=2, e=2),
@@ -156,7 +172,7 @@ def tile_gptqlazyblockcompensatedoutput_x2_kernel(
 
         wnt = {}
 
-        def wn_turn(i, g):
+        def wn_turn(i, g, copy=nc.scalar.copy):
             h = i // 2
             if (h, g) not in wnt:
                 wnt_t = ring.tile([P, 512, 4], BF16, name="wnt", align_bytes=64)
@@ -165,7 +181,7 @@ def tile_gptqlazyblockcompensatedoutput_x2_kernel(
             bank = transposes(words, [[((a * 2 + g) * 2 + uu) * P for a in range(2)] for uu in range(2)], 1)
             b = i % 2
             dst = wnt[(h, g)][:, b * 256 : (b + 1) * 256, :].rearrange("p c t -> p (c t)").bitcast(F32)
-            nc.scalar.copy(
+            copy(
                 out=dst.rearrange("p (r a u) -> p r a u", a=2, u=2),
                 in_=bank[:].rearrange("p u a r -> p r a u"),
             )
@@ -176,17 +192,17 @@ def tile_gptqlazyblockcompensatedoutput_x2_kernel(
 
         xt = {}
 
-        def xr_turn(i):
-            xt_t = ring.tile([P, 2, 256, 4], BF16, name="xt", align_bytes=64)
-            xt[i] = xt_t
+        def xr_turn(i, g):
+            if i not in xt:
+                xt_t = ring.tile([P, 2, 256, 4], BF16, name="xt", align_bytes=64)
+                xt[i] = xt_t
             words = xr_sb[i][:].rearrange("p a k -> p (a k)").bitcast(F32)
-            for g in range(2):
-                bank = transposes(words, [[a * 512 + g * 256 + uu for a in range(2)] for uu in range(2)], 2)
-                dst = xt_t[:, g, :, :].rearrange("p c t -> p (c t)").bitcast(F32)
-                nc.scalar.copy(
-                    out=dst.rearrange("p (r a u) -> p r a u", a=2, u=2),
-                    in_=bank[:].rearrange("p u a r -> p r a u"),
-                )
+            bank = transposes(words, [[a * 512 + g * 256 + uu for a in range(2)] for uu in range(2)], 2)
+            dst = xt[i][:, g, :, :].rearrange("p c t -> p (c t)").bitcast(F32)
+            nc.scalar.copy(
+                out=dst.rearrange("p (r a u) -> p r a u", a=2, u=2),
+                in_=bank[:].rearrange("p u a r -> p r a u"),
+            )
 
         def xr_quant(i):
             quant(
@@ -200,7 +216,7 @@ def tile_gptqlazyblockcompensatedoutput_x2_kernel(
         def xb_turn(i):
             h, b = i // 2, i % 2
             if b == 0:
-                xbt_t = ring.tile([P, 512, 4], BF16, name="xbt", align_bytes=64)
+                xbt_t = ring.tile([P, 512, 4], BF16, name="xbt", align_bytes=64, bufs=2)
                 xbt[h] = xbt_t
             words = xb_sb[h][:].rearrange("p b a k -> p (b a k)").bitcast(F32)
             bank = transposes(words, [[(b * 2 + a) * 256 + uu for a in range(2)] for uu in range(2)], 2)
@@ -221,7 +237,7 @@ def tile_gptqlazyblockcompensatedoutput_x2_kernel(
             tp = t // 2
             if t % 2 == 0:
                 yo_t = ring.tile([P, 2, 512], F32, name="yo", align_bytes=64)
-                yb_t = ring.tile([P, 2, 2, P, 2], BF16, name="yb", align_bytes=64)
+                yb_t = ring.tile([P, 2, 2, P, 2], BF16, name="yb", align_bytes=64, bufs=8)
                 yo[(h, tp)] = yo_t
                 yb[(h, tp)] = yb_t
             n = slice(h * 512, (h + 1) * 512)
@@ -264,11 +280,12 @@ def tile_gptqlazyblockcompensatedoutput_x2_kernel(
         yt = {}
 
         def y_turn(h, tp):
+            copy = nc.scalar.copy if tp % 2 else nc.vector.tensor_copy
             words = yb[(h, tp)][:].rearrange("p t u k e -> p (t u k e)").bitcast(F32)
             bank = transposes(words, [[(t * 2 + uu) * P for t in range(2)] for uu in range(2)], 1)
             yt_t = ring.tile([P, 256, 4], BF16, name="yt", align_bytes=64)
             yt[(h, tp)] = yt_t
-            nc.scalar.copy(
+            copy(
                 out=yt_t[:].rearrange("p c t -> p (c t)").bitcast(F32).rearrange("p (c u) -> p c u", u=2),
                 in_=bank[:].rearrange("p u t r -> p (t r) u"),
             )
@@ -296,70 +313,102 @@ def tile_gptqlazyblockcompensatedoutput_x2_kernel(
                         in_=ps[h][32 * q : 32 * q + 4, :].bitcast(I32),
                     )
 
-        def stage1_block(i):
+        def s(i, g):
+            banks = [stage1(i, a, g) for a in range(2)]
             for a in range(2):
-                for g in range(2):
-                    stage1(i, a, g)
+                sub(i, a, g, banks[a])
 
-        def y_pair(h, tp):
-            y_mm(h, 2 * tp)
-            y_mm(h, 2 * tp + 1)
+        def y(h, ts):
+            for t in ts:
+                y_mm(h, t)
 
-        def y_round_pair(h, tp):
-            y_round(h, 2 * tp)
-            y_round(h, 2 * tp + 1)
+        def yr(h, ts):
+            for t in ts:
+                y_round(h, t)
 
+        vcopy, scopy = nc.vector.tensor_copy, nc.scalar.copy
         with tc.manual_schedule():
-            u_copy(0, 0)
-            u_copy(1, 1)
             e_block(0)
-            e_block(1)
-            u_quant(0)
             e_quant(0)
+            e_block(1)
+            e_quant(1)
+            xr_turn(0, 0)
+            xr_turn(0, 1)
+            u_copy(0, 0, vcopy)
+            u_copy(0, 1, vcopy)
+            u_quant(0)
             e_block(2)
             e_block(3)
-            u_quant(1)
+            e_quant(2)
+            u_copy(1, 1, scopy)
             xb_turn(0)
+            s(0, 0)
+            u_copy(1, 0, vcopy)
+            u_quant(1)
             xb_turn(1)
-            stage1_block(0)
-            xr_turn(0)
-            e_quant(1)
-            xb_quant(0)
-            stage1_block(1)
-            xr_turn(1)
-            wn_turn(0, 0)
-            wn_turn(0, 1)
+            s(1, 0)
+            e_quant(3)
             xr_quant(0)
-            stage1_block(2)
-            xr_turn(2)
-            wn_turn(1, 0)
-            wn_turn(1, 1)
-            xr_quant(1)
-            wn_quant(0, 0)
-            wn_quant(0, 1)
-            stage1_block(3)
-            xr_turn(3)
             xb_turn(2)
             xb_turn(3)
-            xr_quant(2)
-            y_pair(0, 0)
-            wn_turn(2, 0)
-            wn_turn(2, 1)
-            xr_quant(3)
+            wn_turn(0, 0)
+            s(0, 1)
+            s(1, 1)
+            xb_quant(0)
+            xr_turn(1, 0)
+            xr_turn(1, 1)
+            wn_turn(1, 0)
+            s(2, 0)
+            xr_turn(2, 0)
+            s(2, 1)
+            wn_quant(0, 0)
+            wn_turn(0, 1)
+            xr_turn(2, 1)
+            wn_turn(1, 1)
+            wn_quant(0, 1)
+            s(3, 0)
+            xr_quant(1)
             xb_quant(1)
-            y_pair(0, 1)
-            y_round_pair(0, 0)
+            xr_turn(3, 0)
+            xr_turn(3, 1)
+            wn_turn(2, 0)
+            xr_quant(2)
+            y(0, [0, 1])
+            s(3, 1)
+            y(0, [2])
+            yr(0, [0, 1])
+            xr_quant(3)
+            y(0, [3, 4])
+            wn_turn(2, 1)
             wn_turn(3, 0)
             wn_turn(3, 1)
             wn_quant(1, 0)
+            yr(0, [2, 3])
+            y(0, [5, 6, 7])
             wn_quant(1, 1)
-            y_round_pair(0, 1)
-            pairs = [(h, tp) for h in range(2) for tp in range(4)]
-            for j in range(2, 8):
-                y_pair(*pairs[j])
-                y_turn(*pairs[j - 2])
-                y_round_pair(*pairs[j])
-                y_quant(*pairs[j - 2])
-            for j in range(6, 8):
-                y_turn(*pairs[j])
-                y_quant(*pairs[j])
+            yr(0, [4, 5, 6, 7])
+            for t in range(4):
+                y(1, [t])
+                yr(1, [t])
+            for tp in range(2):
+                y_turn(0, tp)
+            for tp in range(2):
+                y_quant(0, tp)
+            for t in (4, 5):
+                y(1, [t])
+                yr(1, [t])
+            y_turn(0, 2)
+            y_turn(0, 3)
+            y_turn(1, 0)
+            y_quant(0, 2)
+            y_quant(0, 3)
+            for t in (6, 7):
+                y(1, [t])
+                yr(1, [t])
+            y_quant(1, 0)
+            y_turn(1, 1)
+            y_quant(1, 1)
+            y_turn(1, 2)
+            y_turn(1, 3)
+            y_quant(1, 2)
+            y_quant(1, 3)

@@ -13,402 +13,415 @@ U32 = mybir.dt.uint32
 U8 = mybir.dt.uint8
 FP8X4 = mybir.dt.float8_e4m3fn_x4
 FP4X4 = mybir.dt.float4_e2m1fn_x4
-SUB = mybir.AluOpType.subtract
-MULT = mybir.AluOpType.mult
 
 P = 128
+BANK = 512
+BLOCK = 256
+
+
+def flat(ap):
+    names = ["d%d" % i for i in range(ap.ndim - 1)]
+    return ap.rearrange("p %s -> p (%s)" % (" ".join(names), " ".join(names)))
 
 
 def tile_gptqlazyblockcompensatedoutput_x2_kernel(
     tc, delta, rd, u, wr, q_words, q_scales, xb, xr, out_0, out_1, out_2
 ):
     nc = tc.nc
+    vcopy, scopy = nc.vector.tensor_copy, nc.scalar.copy
     with ExitStack() as ctx:
         keep = ctx.enter_context(tc.tile_pool(name="keep", bufs=1))
         ring = ctx.enter_context(tc.tile_pool(name="ring", bufs=4))
-        tps = ctx.enter_context(tc.psum_pool(name="tps", bufs=3))
-        acc = ctx.enter_context(tc.psum_pool(name="acc", bufs=5))
+        tps = ctx.enter_context(tc.psum_pool(name="tps", bufs=4))
+        acc = ctx.enter_context(tc.psum_pool(name="acc", bufs=4))
 
         def tl(shape, dt, nm):
             t = keep.tile(shape, dt, name=nm, align_bytes=64)
             return t
 
-        q_plane = tl([P, N], U8, "q_plane")
-        nc.gpsimd.memset(q_plane[:].bitcast(I32), 0)
+        q_s = tl([P, N], U8, "q_s")
+        nc.gpsimd.memset(q_s[:].bitcast(I32), 0)
         ident = tl([P, P], F32, "ident")
         make_identity(nc, ident[:])
 
-        rd4 = tl([P, 1, 2, 2], BF16, "rd4")
-        d_sb = [tl([P, 2, 2, B], BF16, "d_sb%d" % h) for h in range(2)]
-        u_sb = [tl([P, 4, 512], BF16, "u_sb%d" % h) for h in range(2)]
-        wr_sb = [tl([P, 2, R], BF16, "wr_sb%d" % i) for i in range(4)]
-        xr_sb = [tl([P, 2, R], BF16, "xr_sb%d" % i) for i in range(4)]
-        xb_sb = [tl([P, 2, 2, B], BF16, "xb_sb%d" % h) for h in range(2)]
-        q_w = tl([P, 2 * N], U8, "q_w")
+        rd_col = tl([P, 1, 2, 2], BF16, "rd_col")
+        d_in = [tl([P, 2, B], BF16, "d_in%d" % i) for i in range(4)]
+        u_in = [tl([P, 4, BANK], BF16, "u_in%d" % g) for g in range(2)]
+        wr_in = [tl([P, 2, R], BF16, "wr_in%d" % i) for i in range(4)]
+        xr_in = [tl([P, 2, R], BF16, "xr_in%d" % i) for i in range(4)]
+        xb_in = [tl([P, 2, 2, B], BF16, "xb_in%d" % h) for h in range(2)]
+        q_c = tl([P, 2 * N], U8, "q_c")
 
-        def load_half(dst, src, h):
-            nc.sync.dma_start(
-                out=dst[:],
-                in_=src[h * 512 : (h + 1) * 512, :].rearrange("(b p a) k -> p b a k", p=P, a=2),
-            )
+        e_g = [tl([P, BLOCK, 4], BF16, "e_g%d" % i) for i in range(4)]
+        u_g = [tl([P, BANK, 4], BF16, "u_g%d" % g) for g in range(2)]
+        xb_g = [tl([P, 2 * BLOCK, 4], BF16, "xb_g%d" % h) for h in range(2)]
+        xr_g = [tl([P, 2, BLOCK, 4], BF16, "xr_g%d" % i) for i in range(4)]
+        wn_r = [tl([P, 2, 2, 2, P, 2], BF16, "wn_r%d" % i) for i in range(4)]
+        wn_g = [[tl([P, BANK, 4], BF16, "wn_g%d%d" % (h, g)) for g in range(2)] for h in range(2)]
 
-        def load_block(dst, src, i):
-            nc.sync.dma_start(
-                out=dst[:], in_=src[i * 256 : (i + 1) * 256, :].rearrange("(p a) k -> p a k", a=2)
-            )
-
-        u_view = u.rearrange("(p j) r -> p j r", j=4)
-
-        nc.scalar.dma_start(
-            out=rd4[:].rearrange("p o u e -> p (o u e)"), in_=rd.rearrange("(p t) -> p t", t=4)
-        )
-        def load_u(g):
-            nc.sync.dma_start(out=u_sb[g][:], in_=u_view[:, :, g * 512 : (g + 1) * 512])
-
-        def load_d(i):
-            h, b = i // 2, i % 2
-            nc.sync.dma_start(
-                out=d_sb[h][:, b, :, :],
-                in_=delta[i * 256 : (i + 1) * 256, :].rearrange("(p a) k -> p a k", a=2),
-            )
-
-        for q in range(4):
-            nc.scalar.dma_start(
-                out=q_plane[32 * q : 32 * q + 4, :].bitcast(I32),
-                in_=q_scales[0, 4 * q : 4 * q + 4, :].bitcast(I32),
-            )
-        load_d(0)
-        load_d(1)
-        load_block(xr_sb[0], xr, 0)
-        load_u(0)
-        load_half(d_sb[1], delta, 1)
-        load_half(xb_sb[0], xb, 0)
-        load_u(1)
-        load_block(wr_sb[0], wr, 0)
-        load_half(xb_sb[1], xb, 1)
-        load_block(wr_sb[1], wr, 1)
-        load_block(xr_sb[1], xr, 1)
-        load_block(wr_sb[2], wr, 2)
-        load_block(xr_sb[2], xr, 2)
-        load_block(xr_sb[3], xr, 3)
-        nc.sync.dma_start(out=q_w[:].bitcast(I32), in_=q_words[0].bitcast(I32))
-        load_block(wr_sb[3], wr, 3)
-
-        eg = [tl([P, 512, 4], BF16, "eg%d" % h) for h in range(2)]
-        ug = [tl([P, 512, 4], BF16, "ug%d" % h) for h in range(2)]
-        wn = [tl([P, 2, 2, 2, P, 2], BF16, "wn%d" % i) for i in range(4)]
-        e_c = tl([P, N], U32, "e_c")
-        e_s = tl([P, N], U8, "e_s")
-        u_c = tl([P, R], U32, "u_c")
-        u_s = tl([P, R], U8, "u_s")
+        e_c, e_s = tl([P, N], U32, "e_c"), tl([P, N], U8, "e_s")
+        u_c, u_s = tl([P, R], U32, "u_c"), tl([P, R], U8, "u_s")
+        xb_c, xb_s = tl([P, T], U32, "xb_c"), tl([P, T], U8, "xb_s")
+        xr_c = [tl([P, 2, BLOCK], U32, "xr_c%d" % i) for i in range(4)]
+        xr_s = [tl([P, 2, BLOCK], U8, "xr_s%d" % i) for i in range(4)]
         wn_c = [tl([P, N], U32, "wn_c%d" % g) for g in range(2)]
         wn_s = [tl([P, N], U8, "wn_s%d" % g) for g in range(2)]
-        xr_c = [tl([P, 2, 256], U32, "xr_c%d" % i) for i in range(4)]
-        xr_s = [tl([P, 2, 256], U8, "xr_s%d" % i) for i in range(4)]
-        xb_c = tl([P, T], U32, "xb_c")
-        xb_s = tl([P, T], U8, "xb_s")
+        p_s = tl([P, 2, T], U8, "p_s")
+
+        nc.scalar.dma_start(out=flat(rd_col[:]), in_=rd.rearrange("(p t) -> p t", t=4))
+        for q in range(4):
+            nc.scalar.dma_start(
+                out=q_s[32 * q : 32 * q + 4, :].bitcast(I32),
+                in_=q_scales[0, 4 * q : 4 * q + 4, :].bitcast(I32),
+            )
+
+        def load_block(tile, src, i):
+            rows = src[i * BLOCK : (i + 1) * BLOCK, :]
+            nc.sync.dma_start(out=tile[:], in_=rows.rearrange("(p a) k -> p a k", a=2))
+
+        def load_u(g):
+            cols = u.rearrange("(p j) r -> p j r", j=4)[:, :, g * BANK : (g + 1) * BANK]
+            nc.sync.dma_start(out=u_in[g][:], in_=cols)
+
+        def load_xb(h):
+            rows = xb[h * 512 : (h + 1) * 512, :]
+            nc.sync.dma_start(out=xb_in[h][:], in_=rows.rearrange("(b p a) k -> p b a k", p=P, a=2))
+
+        load_block(d_in[0], delta, 0)
+        load_block(d_in[1], delta, 1)
+        load_u(0)
+        load_block(d_in[2], delta, 2)
+        load_block(d_in[3], delta, 3)
+        load_xb(0)
+        load_u(1)
+        load_block(xr_in[0], xr, 0)
+        load_block(wr_in[0], wr, 0)
+        load_xb(1)
+        load_block(wr_in[1], wr, 1)
+        load_block(xr_in[1], xr, 1)
+        load_block(xr_in[2], xr, 2)
+        load_block(wr_in[2], wr, 2)
+        load_block(xr_in[3], xr, 3)
+        nc.sync.dma_start(out=q_c[:].bitcast(I32), in_=q_words[0].bitcast(I32))
+        load_block(wr_in[3], wr, 3)
 
         def quant(src, codes, scales):
             nc.vector.quantize_mx(out=codes.bitcast(FP8X4), scales=scales, in_=src)
 
-        def transposes(words, offsets, step):
-            bank = tps.tile([P, 2, 2, P], F32, name="tp")
-            for uu in range(2):
-                for a in range(2):
-                    o = offsets[uu][a]
-                    nc.tensor.transpose(
-                        bank[:, uu, a, :], words[:, o : o + P * step - step + 1 : step], ident[:]
-                    )
-            return bank
+        banks = {}
 
-        def e_block(i):
-            h, b = i // 2, i % 2
-            words = d_sb[h][:].rearrange("p b a k -> p (b a k)").bitcast(F32)
-            bank = transposes(words, [[(b * 2 + a) * 256 + uu for a in range(2)] for uu in range(2)], 2)
+        def turn(key, tile, first, step):
+            words = flat(tile[:]).bitcast(F32)
+            na = len(first[0])
+            bank = tps.tile([P, 2, na, P], F32, name="turned")
+            for uu in range(2):
+                for a in range(na):
+                    o = first[uu][a]
+                    nc.tensor.transpose(bank[:, uu, a, :], words[:, o : o + (P - 1) * step + 1 : step], ident[:])
+            banks[key] = bank
+
+        def unload(key, dst, copy):
+            copy(
+                out=flat(dst).bitcast(F32).rearrange("p (r a u) -> p r a u", a=2, u=2),
+                in_=banks[key][:].rearrange("p u a r -> p r a u"),
+            )
+
+        def e_turn(i):
+            turn(("e", i), d_in[i], [[a * 256 + uu for a in range(2)] for uu in range(2)], 2)
+
+        def e_scale(i):
+            pairs = flat(banks[("e", i)][:]).bitcast(BF16)
             nc.vector.tensor_tensor(
-                out=eg[h][:, b * 256 : (b + 1) * 256, :].rearrange("p c (u e) -> p c u e", u=2),
-                in0=bank[:].rearrange("p u a r -> p (u a r)").bitcast(BF16).rearrange("p (u c e) -> p c u e", u=2, e=2),
-                in1=rd4[:].to_broadcast([P, 256, 2, 2]),
-                op=MULT,
+                out=e_g[i][:].rearrange("p c (u e) -> p c u e", u=2),
+                in0=pairs.rearrange("p (u c e) -> p c u e", u=2, e=2),
+                in1=rd_col[:].to_broadcast([P, BLOCK, 2, 2]),
+                op=mybir.AluOpType.mult,
             )
 
         def e_quant(i):
-            h, b = i // 2, i % 2
-            s = slice(i * 256, (i + 1) * 256)
-            quant(eg[h][:, b * 256 : (b + 1) * 256, :].rearrange("p c t -> p (c t)"), e_c[:, s], e_s[:, s])
+            s = slice(i * BLOCK, (i + 1) * BLOCK)
+            quant(flat(e_g[i][:]), e_c[:, s], e_s[:, s])
 
         def u_copy(g, b, copy):
             c = slice(b * 256, (b + 1) * 256)
             copy(
-                out=ug[g][:, c, :].rearrange("p (c i) t -> p c t i", i=4),
-                in_=u_sb[g][:, :, c].rearrange("p t (c i) -> p c t i", i=4),
+                out=u_g[g][:, c, :].rearrange("p (c i) t -> p c t i", i=4),
+                in_=u_in[g][:, :, c].rearrange("p t (c i) -> p c t i", i=4),
             )
 
         def u_quant(g):
-            s = slice(g * 512, (g + 1) * 512)
-            quant(ug[g][:].rearrange("p c t -> p (c t)"), u_c[:, s], u_s[:, s])
+            s = slice(g * BANK, (g + 1) * BANK)
+            quant(flat(u_g[g][:]), u_c[:, s], u_s[:, s])
 
-        def stage1(i, a, g):
-            n0 = i * 256 + a * 128
-            bank = acc.tile([P, 512], F32, name="acc")
-            nc.tensor.matmul_mx(
-                out=bank[:],
-                lhsT=e_c[:, n0 : n0 + P].bitcast(FP8X4),
-                lhsT_scale=e_s[:, n0 : n0 + P],
-                rhs=u_c[:, g * 512 : (g + 1) * 512].bitcast(FP8X4),
-                rhs_scale=u_s[:, g * 512 : (g + 1) * 512],
-                start=True,
-                stop=True,
-            )
-            return bank
+        def c_mm(i, g):
+            r = slice(g * BANK, (g + 1) * BANK)
+            for a in range(2):
+                n = slice(i * BLOCK + a * P, i * BLOCK + (a + 1) * P)
+                bank = acc.tile([P, BANK], F32, name="sums")
+                nc.tensor.matmul_mx(
+                    out=bank[:],
+                    lhsT=e_c[:, n].bitcast(FP8X4),
+                    lhsT_scale=e_s[:, n],
+                    rhs=u_c[:, r].bitcast(FP8X4),
+                    rhs_scale=u_s[:, r],
+                    start=True,
+                    stop=True,
+                )
+                banks[("c", i, g, a)] = bank
 
-        def sub(i, a, g, bank):
-            nc.vector.tensor_tensor(
-                out=wn[i][:, a, g, :, :, :],
-                in0=wr_sb[i][:, a, g * 512 : (g + 1) * 512].rearrange("p (k u e) -> p u k e", u=2, e=2),
-                in1=bank[:].rearrange("p (k u e) -> p u k e", u=2, e=2),
-                op=SUB,
-            )
+        def wn_sub(i, g):
+            for a in range(2):
+                nc.vector.tensor_tensor(
+                    out=wn_r[i][:, a, g, :, :, :],
+                    in0=wr_in[i][:, a, g * BANK : (g + 1) * BANK].rearrange("p (k u e) -> p u k e", u=2, e=2),
+                    in1=banks[("c", i, g, a)][:].rearrange("p (k u e) -> p u k e", u=2, e=2),
+                    op=mybir.AluOpType.subtract,
+                )
 
-        wnt = {}
+        def wn_turn(i, g):
+            turn(("wn", i, g), wn_r[i], [[((a * 2 + g) * 2 + uu) * P for a in range(2)] for uu in range(2)], 1)
 
-        def wn_turn(i, g, copy=nc.scalar.copy):
-            h = i // 2
-            if (h, g) not in wnt:
-                wnt_t = ring.tile([P, 512, 4], BF16, name="wnt", align_bytes=64)
-                wnt[(h, g)] = wnt_t
-            words = wn[i][:].rearrange("p a g u k e -> p (a g u k e)").bitcast(F32)
-            bank = transposes(words, [[((a * 2 + g) * 2 + uu) * P for a in range(2)] for uu in range(2)], 1)
+        def wn_unload(i, g, copy):
             b = i % 2
-            dst = wnt[(h, g)][:, b * 256 : (b + 1) * 256, :].rearrange("p c t -> p (c t)").bitcast(F32)
-            copy(
-                out=dst.rearrange("p (r a u) -> p r a u", a=2, u=2),
-                in_=bank[:].rearrange("p u a r -> p r a u"),
-            )
+            unload(("wn", i, g), wn_g[i // 2][g][:, b * BLOCK : (b + 1) * BLOCK, :], copy)
 
         def wn_quant(h, g):
-            s = slice(h * 512, (h + 1) * 512)
-            quant(wnt[(h, g)][:].rearrange("p c t -> p (c t)"), wn_c[g][:, s], wn_s[g][:, s])
-
-        xt = {}
+            s = slice(h * BANK, (h + 1) * BANK)
+            quant(flat(wn_g[h][g][:]), wn_c[g][:, s], wn_s[g][:, s])
 
         def xr_turn(i, g):
-            if i not in xt:
-                xt_t = ring.tile([P, 2, 256, 4], BF16, name="xt", align_bytes=64)
-                xt[i] = xt_t
-            words = xr_sb[i][:].rearrange("p a k -> p (a k)").bitcast(F32)
-            bank = transposes(words, [[a * 512 + g * 256 + uu for a in range(2)] for uu in range(2)], 2)
-            dst = xt[i][:, g, :, :].rearrange("p c t -> p (c t)").bitcast(F32)
-            nc.scalar.copy(
-                out=dst.rearrange("p (r a u) -> p r a u", a=2, u=2),
-                in_=bank[:].rearrange("p u a r -> p r a u"),
-            )
+            turn(("xr", i, g), xr_in[i], [[a * 512 + g * 256 + uu for a in range(2)] for uu in range(2)], 2)
+            unload(("xr", i, g), xr_g[i][:, g, :, :], scopy)
 
         def xr_quant(i):
-            quant(
-                xt[i][:].rearrange("p g c t -> p (g c t)"),
-                xr_c[i][:].rearrange("p g c -> p (g c)"),
-                xr_s[i][:].rearrange("p g c -> p (g c)"),
-            )
+            quant(flat(xr_g[i][:]), flat(xr_c[i][:]), flat(xr_s[i][:]))
 
-        xbt = {}
+        def xb_turn_only(i):
+            h, b = i // 2, i % 2
+            turn(("xb", i), xb_in[h], [[(b * 2 + a) * 256 + uu for a in range(2)] for uu in range(2)], 2)
+
+        def xb_unload(i):
+            h, b = i // 2, i % 2
+            unload(("xb", i), xb_g[h][:, b * BLOCK : (b + 1) * BLOCK, :], scopy)
 
         def xb_turn(i):
-            h, b = i // 2, i % 2
-            if b == 0:
-                xbt_t = ring.tile([P, 512, 4], BF16, name="xbt", align_bytes=64, bufs=2)
-                xbt[h] = xbt_t
-            words = xb_sb[h][:].rearrange("p b a k -> p (b a k)").bitcast(F32)
-            bank = transposes(words, [[(b * 2 + a) * 256 + uu for a in range(2)] for uu in range(2)], 2)
-            dst = xbt[h][:, b * 256 : (b + 1) * 256, :].rearrange("p c t -> p (c t)").bitcast(F32)
-            nc.scalar.copy(
-                out=dst.rearrange("p (r a u) -> p r a u", a=2, u=2),
-                in_=bank[:].rearrange("p u a r -> p r a u"),
-            )
+            xb_turn_only(i)
+            xb_unload(i)
 
         def xb_quant(h):
             s = slice(h * 512, (h + 1) * 512)
-            quant(xbt[h][:].rearrange("p c t -> p (c t)"), xb_c[:, s], xb_s[:, s])
+            quant(flat(xb_g[h][:]), xb_c[:, s], xb_s[:, s])
 
-        yo, yb, pc = {}, {}, {}
-        ps = [tl([P, T], U8, "ps%d" % h) for h in range(2)]
+        y32, y16, p_g, p_c = {}, {}, {}, {}
 
         def y_mm(h, t):
-            tp = t // 2
-            if t % 2 == 0:
-                yo_t = ring.tile([P, 2, 512], F32, name="yo", align_bytes=64)
-                yb_t = ring.tile([P, 2, 2, P, 2], BF16, name="yb", align_bytes=64, bufs=8)
-                yo[(h, tp)] = yo_t
-                yb[(h, tp)] = yb_t
-            n = slice(h * 512, (h + 1) * 512)
-            bank = acc.tile([P, 512], F32, name="acc")
+            n = slice(h * BANK, (h + 1) * BANK)
+            bank = acc.tile([P, BANK], F32, name="sums")
             nc.tensor.matmul_mx(
                 out=bank[:],
                 lhsT=xb_c[:, t * P : (t + 1) * P].bitcast(FP8X4),
                 lhsT_scale=xb_s[:, t * P : (t + 1) * P],
-                rhs=q_w[:, h * 1024 : (h + 1) * 1024].bitcast(FP4X4),
-                rhs_scale=q_plane[:, n],
+                rhs=q_c[:, 2 * h * BANK : 2 * (h + 1) * BANK].bitcast(FP4X4),
+                rhs_scale=q_s[:, n],
                 start=True,
                 stop=False,
             )
-            c0 = (t % 2) * P
+            tp, b = t // 2, t % 2
+            c = slice(b * P, (b + 1) * P)
             for g in range(2):
                 nc.tensor.matmul_mx(
                     out=bank[:],
-                    lhsT=xr_c[tp][:, g, c0 : c0 + P].bitcast(FP8X4),
-                    lhsT_scale=xr_s[tp][:, g, c0 : c0 + P],
+                    lhsT=xr_c[tp][:, g, c].bitcast(FP8X4),
+                    lhsT_scale=xr_s[tp][:, g, c],
                     rhs=wn_c[g][:, n].bitcast(FP8X4),
                     rhs_scale=wn_s[g][:, n],
                     start=False,
                     stop=(g == 1),
                 )
-            nc.scalar.copy(out=yo[(h, tp)][:, t % 2, :], in_=bank[:])
+            if b == 0:
+                y32_t = ring.tile([P, 2, BANK], F32, name="y32", align_bytes=64)
+                y16_t = ring.tile([P, 2, 2, P, 2], BF16, name="y16", align_bytes=64, bufs=8)
+                y32[(h, tp)] = y32_t
+                y16[(h, tp)] = y16_t
+            nc.scalar.copy(out=y32[(h, tp)][:, b, :], in_=bank[:])
+            banks[("y", h, t)] = bank
 
-        def y_round(h, t):
-            tp = t // 2
-            n = slice(h * 512, (h + 1) * 512)
+        def y_round(h, t, src=None):
+            tp, b = t // 2, t % 2
+            src = y32[(h, tp)][:, b, :] if src is None else src
             nc.vector.tensor_copy(
-                out=yb[(h, tp)][:, t % 2, :, :, :],
-                in_=yo[(h, tp)][:, t % 2, :].rearrange("p (k u e) -> p u k e", u=2, e=2),
+                out=y16[(h, tp)][:, b, :, :, :], in_=src.rearrange("p (k u e) -> p u k e", u=2, e=2)
             )
-            if t % 2 == 1:
-                nc.sync.dma_start(
-                    out=out_0[tp * 256 : (tp + 1) * 256, n].rearrange("(t p) n -> p t n", p=P),
-                    in_=yo[(h, tp)][:],
-                )
 
-        yt = {}
+        def y_store(h, tp):
+            rows = out_0[tp * BLOCK : (tp + 1) * BLOCK, h * BANK : (h + 1) * BANK]
+            nc.sync.dma_start(out=rows.rearrange("(b p) n -> p b n", p=P), in_=y32[(h, tp)][:])
 
-        def y_turn(h, tp):
-            copy = nc.scalar.copy if tp % 2 else nc.vector.tensor_copy
-            words = yb[(h, tp)][:].rearrange("p t u k e -> p (t u k e)").bitcast(F32)
-            bank = transposes(words, [[(t * 2 + uu) * P for t in range(2)] for uu in range(2)], 1)
-            yt_t = ring.tile([P, 256, 4], BF16, name="yt", align_bytes=64)
-            yt[(h, tp)] = yt_t
+        def p_turn(h, tiles):
+            tp = tiles[0] // 2
+            first = [[((t % 2) * 2 + uu) * P for t in tiles] for uu in range(2)]
+            turn(("p", h, tiles[0]), y16[(h, tp)], first, 1)
+
+        def p_unload(h, tiles, copy):
+            w = len(tiles) * P
+            p_g_t = ring.tile([P, BLOCK, 4], BF16, name="p_g", align_bytes=64)
+            p_g[(h, tiles[0])] = p_g_t
             copy(
-                out=yt_t[:].rearrange("p c t -> p (c t)").bitcast(F32).rearrange("p (c u) -> p c u", u=2),
-                in_=bank[:].rearrange("p u t r -> p (t r) u"),
+                out=flat(p_g_t[:, :w, :]).bitcast(F32).rearrange("p (c u) -> p c u", u=2),
+                in_=banks[("p", h, tiles[0])][:].rearrange("p u b r -> p (b r) u"),
             )
 
-        def y_quant(h, tp):
-            th = tp // 2
-            if tp % 2 == 0:
-                pc_t = ring.tile([P, 512], U32, name="pc", align_bytes=64)
-                pc[(h, th)] = pc_t
-            c = (tp % 2) * 256
+        def p_quant(h, tiles):
+            half = tiles[0] // 4
+            w = len(tiles) * P
+            if (h, half) not in p_c:
+                p_c_t = ring.tile([P, 512], U32, name="p_c", align_bytes=64)
+                p_c[(h, half)] = p_c_t
+            c = tiles[0] * P - half * 512
             quant(
-                yt[(h, tp)][:].rearrange("p c t -> p (c t)"),
-                pc[(h, th)][:, c : c + 256],
-                ps[h][:, tp * 256 : (tp + 1) * 256],
+                flat(p_g[(h, tiles[0])][:, :w, :]),
+                p_c[(h, half)][:, c : c + w],
+                p_s[:, h, tiles[0] * P : tiles[0] * P + w],
             )
-            if tp % 2 == 1:
+
+        def codes_store(h, t0, t1):
+            half = t0 // 4
+            cols = out_1[h, :, t0 * P : t1 * P, :]
+            nc.sync.dma_start(
+                out=cols.rearrange("p m t -> p (m t)").bitcast(I32),
+                in_=p_c[(h, half)][:, (t0 - 4 * half) * P : (t1 - 4 * half) * P].bitcast(I32),
+            )
+
+        def scales_store():
+            for q in range(4):
+                rows = out_2.bitcast(I32)[:, 4 * q : 4 * q + 4, :]
                 nc.sync.dma_start(
-                    out=out_1[h, :, th * 512 : (th + 1) * 512, :].rearrange("p m t -> p (m t)").bitcast(I32),
-                    in_=pc[(h, th)][:].bitcast(I32),
+                    out=rows.rearrange("h r t -> r h t"),
+                    in_=p_s[32 * q : 32 * q + 4, :, :].bitcast(I32),
                 )
-            if tp == 3:
-                for q in range(4):
-                    nc.sync.dma_start(
-                        out=out_2[h, 4 * q : 4 * q + 4, :].bitcast(I32),
-                        in_=ps[h][32 * q : 32 * q + 4, :].bitcast(I32),
-                    )
 
-        def s(i, g):
-            banks = [stage1(i, a, g) for a in range(2)]
-            for a in range(2):
-                sub(i, a, g, banks[a])
-
-        def y(h, ts):
-            for t in ts:
-                y_mm(h, t)
-
-        def yr(h, ts):
-            for t in ts:
-                y_round(h, t)
-
-        vcopy, scopy = nc.vector.tensor_copy, nc.scalar.copy
         with tc.manual_schedule():
-            e_block(0)
-            e_quant(0)
-            e_block(1)
-            e_quant(1)
-            xr_turn(0, 0)
-            xr_turn(0, 1)
-            u_copy(0, 0, vcopy)
+            e_turn(0)
+            e_scale(0)
+            e_turn(1)
+            e_scale(1)
+            u_copy(0, 0, scopy)
             u_copy(0, 1, vcopy)
+            e_quant(0)
+            e_turn(2)
+            e_scale(2)
             u_quant(0)
-            e_block(2)
-            e_block(3)
-            e_quant(2)
+            e_quant(1)
             u_copy(1, 1, scopy)
-            xb_turn(0)
-            s(0, 0)
             u_copy(1, 0, vcopy)
+            e_turn(3)
+            e_scale(3)
             u_quant(1)
+            xb_turn(0)
             xb_turn(1)
-            s(1, 0)
+            c_mm(0, 0)
+            wn_sub(0, 0)
+            xr_turn(0, 0)
+            c_mm(0, 1)
+            wn_sub(0, 1)
+            xr_turn(0, 1)
+            xb_turn(2)
+            e_quant(2)
+            c_mm(1, 1)
+            wn_sub(1, 1)
+            c_mm(1, 0)
+            wn_sub(1, 0)
+            wn_turn(0, 0)
+            wn_unload(0, 0, scopy)
+            wn_turn(0, 1)
+            wn_unload(0, 1, scopy)
             e_quant(3)
             xr_quant(0)
-            xb_turn(2)
-            xb_turn(3)
-            wn_turn(0, 0)
-            s(0, 1)
-            s(1, 1)
-            xb_quant(0)
+            xb_turn_only(3)
+            c_mm(2, 1)
+            wn_sub(2, 1)
+            wn_turn(1, 1)
+            wn_unload(1, 1, scopy)
+            xb_unload(3)
             xr_turn(1, 0)
             xr_turn(1, 1)
-            wn_turn(1, 0)
-            s(2, 0)
-            xr_turn(2, 0)
-            s(2, 1)
-            wn_quant(0, 0)
-            wn_turn(0, 1)
-            xr_turn(2, 1)
-            wn_turn(1, 1)
+            xb_quant(0)
             wn_quant(0, 1)
-            s(3, 0)
-            xr_quant(1)
-            xb_quant(1)
+            c_mm(2, 0)
+            wn_sub(2, 0)
+            xr_turn(2, 0)
+            wn_turn(1, 0)
+            wn_unload(1, 0, scopy)
+            xr_turn(2, 1)
+            wn_quant(0, 0)
+            c_mm(3, 1)
+            wn_sub(3, 1)
             xr_turn(3, 0)
             xr_turn(3, 1)
-            wn_turn(2, 0)
+            c_mm(3, 0)
+            wn_sub(3, 0)
+            xr_quant(1)
             xr_quant(2)
-            y(0, [0, 1])
-            s(3, 1)
-            y(0, [2])
-            yr(0, [0, 1])
+            for t in range(2):
+                y_mm(0, t)
+            xb_quant(1)
+            for i in (2, 3):
+                for g in range(2):
+                    wn_turn(i, g)
+            wn_unload(2, 0, scopy)
+            wn_unload(2, 1, scopy)
+            wn_unload(3, 1, scopy)
+            y_round(0, 0)
             xr_quant(3)
-            y(0, [3, 4])
-            wn_turn(2, 1)
-            wn_turn(3, 0)
-            wn_turn(3, 1)
-            wn_quant(1, 0)
-            yr(0, [2, 3])
-            y(0, [5, 6, 7])
+            wn_unload(3, 0, vcopy)
             wn_quant(1, 1)
-            yr(0, [4, 5, 6, 7])
-            for t in range(4):
-                y(1, [t])
-                yr(1, [t])
-            for tp in range(2):
-                y_turn(0, tp)
-            for tp in range(2):
-                y_quant(0, tp)
-            for t in (4, 5):
-                y(1, [t])
-                yr(1, [t])
-            y_turn(0, 2)
-            y_turn(0, 3)
-            y_turn(1, 0)
-            y_quant(0, 2)
-            y_quant(0, 3)
-            for t in (6, 7):
-                y(1, [t])
-                yr(1, [t])
-            y_quant(1, 0)
-            y_turn(1, 1)
-            y_quant(1, 1)
-            y_turn(1, 2)
-            y_turn(1, 3)
-            y_quant(1, 2)
-            y_quant(1, 3)
+            wn_quant(1, 0)
+            y_round(0, 1)
+            y_store(0, 0)
+            for t in range(2, 8):
+                y_mm(0, t)
+                y_round(0, t)
+                if t % 2 == 1:
+                    y_store(0, t // 2)
+            for t in range(3):
+                y_mm(1, t)
+            y_round(1, 0)
+            y_round(1, 1)
+            y_store(1, 0)
+            pairs = [(2 * tp, 2 * tp + 1) for tp in range(4)]
+            for tp in range(3):
+                p_turn(0, pairs[tp])
+            for tp in range(3):
+                p_unload(0, pairs[tp], vcopy if tp == 1 else scopy)
+            for tp in range(3):
+                p_quant(0, pairs[tp])
+            codes_store(0, 0, 4)
+            y_round(1, 2)
+            for t in range(3, 8):
+                y_mm(1, t)
+                y_round(1, t, banks[("y", 1, t)][:] if t > 5 else None)
+                if t % 2 == 1:
+                    y_store(1, t // 2)
+            p_turn(0, pairs[3])
+            p_unload(0, pairs[3], scopy)
+            p_turn(1, pairs[0])
+            p_unload(1, pairs[0], scopy)
+            p_turn(1, pairs[1])
+            p_unload(1, pairs[1], vcopy)
+            p_quant(0, pairs[3])
+            codes_store(0, 4, 8)
+            p_turn(1, pairs[2])
+            p_unload(1, pairs[2], scopy)
+            p_turn(1, (6,))
+            p_unload(1, (6,), scopy)
+            p_quant(1, pairs[0])
+            p_quant(1, pairs[1])
+            codes_store(1, 0, 4)
+            p_turn(1, (7,))
+            p_unload(1, (7,), scopy)
+            p_quant(1, pairs[2])
+            p_quant(1, (6,))
+            codes_store(1, 4, 7)
+            p_quant(1, (7,))
+            codes_store(1, 7, 8)
+            scales_store()

from contextlib import ExitStack

import concourse.mybir as mybir
from concourse.masks import make_identity

N, B, R, T = 1024, 512, 1024, 1024
FLOPS = 2 * (N * B * R + T * R * N + T * B * N)

F32 = mybir.dt.float32
BF16 = mybir.dt.bfloat16
I32 = mybir.dt.int32
U32 = mybir.dt.uint32
U8 = mybir.dt.uint8
FP8X4 = mybir.dt.float8_e4m3fn_x4
FP4X4 = mybir.dt.float4_e2m1fn_x4

P = 128
BANK = 512
BLOCK = 256


def flat(ap):
    names = ["d%d" % i for i in range(ap.ndim - 1)]
    return ap.rearrange("p %s -> p (%s)" % (" ".join(names), " ".join(names)))


def tile_gptqlazyblockcompensatedoutput_x2_kernel(
    tc, delta, rd, u, wr, q_words, q_scales, xb, xr, out_0, out_1, out_2
):
    nc = tc.nc
    vcopy, scopy = nc.vector.tensor_copy, nc.scalar.copy
    with ExitStack() as ctx:
        keep = ctx.enter_context(tc.tile_pool(name="keep", bufs=1))
        ring = ctx.enter_context(tc.tile_pool(name="ring", bufs=4))
        tps = ctx.enter_context(tc.psum_pool(name="tps", bufs=4))
        acc = ctx.enter_context(tc.psum_pool(name="acc", bufs=4))

        def tl(shape, dt, nm):
            t = keep.tile(shape, dt, name=nm, align_bytes=64)
            return t

        q_s = tl([P, N], U8, "q_s")
        nc.gpsimd.memset(q_s[:].bitcast(I32), 0)
        ident = tl([P, P], F32, "ident")
        make_identity(nc, ident[:])

        rd_col = tl([P, 1, 2, 2], BF16, "rd_col")
        d_in = [tl([P, 2, B], BF16, "d_in%d" % i) for i in range(4)]
        u_in = [tl([P, 4, BANK], BF16, "u_in%d" % g) for g in range(2)]
        wr_in = [tl([P, 2, R], BF16, "wr_in%d" % i) for i in range(4)]
        xr_in = [tl([P, 2, R], BF16, "xr_in%d" % i) for i in range(4)]
        xb_in = [tl([P, 2, 2, B], BF16, "xb_in%d" % h) for h in range(2)]
        q_c = tl([P, 2 * N], U8, "q_c")

        e_g = [tl([P, BLOCK, 4], BF16, "e_g%d" % i) for i in range(4)]
        u_g = [tl([P, BANK, 4], BF16, "u_g%d" % g) for g in range(2)]
        xb_g = [tl([P, 2 * BLOCK, 4], BF16, "xb_g%d" % h) for h in range(2)]
        xr_g = [tl([P, 2, BLOCK, 4], BF16, "xr_g%d" % i) for i in range(4)]
        wn_r = [tl([P, 2, 2, 2, P, 2], BF16, "wn_r%d" % i) for i in range(4)]
        wn_g = [[tl([P, BANK, 4], BF16, "wn_g%d%d" % (h, g)) for g in range(2)] for h in range(2)]

        e_c, e_s = tl([P, N], U32, "e_c"), tl([P, N], U8, "e_s")
        u_c, u_s = tl([P, R], U32, "u_c"), tl([P, R], U8, "u_s")
        xb_c, xb_s = tl([P, T], U32, "xb_c"), tl([P, T], U8, "xb_s")
        xr_c = [tl([P, 2, BLOCK], U32, "xr_c%d" % i) for i in range(4)]
        xr_s = [tl([P, 2, BLOCK], U8, "xr_s%d" % i) for i in range(4)]
        wn_c = [tl([P, N], U32, "wn_c%d" % g) for g in range(2)]
        wn_s = [tl([P, N], U8, "wn_s%d" % g) for g in range(2)]
        p_s = tl([P, 2, T], U8, "p_s")

        nc.scalar.dma_start(out=flat(rd_col[:]), in_=rd.rearrange("(p t) -> p t", t=4))
        for q in range(4):
            nc.scalar.dma_start(
                out=q_s[32 * q : 32 * q + 4, :].bitcast(I32),
                in_=q_scales[0, 4 * q : 4 * q + 4, :].bitcast(I32),
            )

        def load_block(tile, src, i):
            rows = src[i * BLOCK : (i + 1) * BLOCK, :]
            nc.sync.dma_start(out=tile[:], in_=rows.rearrange("(p a) k -> p a k", a=2))

        def load_u(g):
            cols = u.rearrange("(p j) r -> p j r", j=4)[:, :, g * BANK : (g + 1) * BANK]
            nc.sync.dma_start(out=u_in[g][:], in_=cols)

        def load_xb(h):
            rows = xb[h * 512 : (h + 1) * 512, :]
            nc.sync.dma_start(out=xb_in[h][:], in_=rows.rearrange("(b p a) k -> p b a k", p=P, a=2))

        load_block(d_in[0], delta, 0)
        load_block(d_in[1], delta, 1)
        load_u(0)
        load_block(d_in[2], delta, 2)
        load_block(d_in[3], delta, 3)
        load_xb(0)
        load_u(1)
        load_block(xr_in[0], xr, 0)
        load_block(wr_in[0], wr, 0)
        load_xb(1)
        load_block(wr_in[1], wr, 1)
        load_block(xr_in[1], xr, 1)
        load_block(xr_in[2], xr, 2)
        load_block(wr_in[2], wr, 2)
        load_block(xr_in[3], xr, 3)
        nc.sync.dma_start(out=q_c[:].bitcast(I32), in_=q_words[0].bitcast(I32))
        load_block(wr_in[3], wr, 3)

        def quant(src, codes, scales):
            nc.vector.quantize_mx(out=codes.bitcast(FP8X4), scales=scales, in_=src)

        banks = {}

        def turn(key, tile, first, step):
            words = flat(tile[:]).bitcast(F32)
            na = len(first[0])
            bank = tps.tile([P, 2, na, P], F32, name="turned")
            for uu in range(2):
                for a in range(na):
                    o = first[uu][a]
                    nc.tensor.transpose(bank[:, uu, a, :], words[:, o : o + (P - 1) * step + 1 : step], ident[:])
            banks[key] = bank

        def unload(key, dst, copy):
            copy(
                out=flat(dst).bitcast(F32).rearrange("p (r a u) -> p r a u", a=2, u=2),
                in_=banks[key][:].rearrange("p u a r -> p r a u"),
            )

        def e_turn(i):
            turn(("e", i), d_in[i], [[a * 256 + uu for a in range(2)] for uu in range(2)], 2)

        def e_scale(i):
            pairs = flat(banks[("e", i)][:]).bitcast(BF16)
            nc.vector.tensor_tensor(
                out=e_g[i][:].rearrange("p c (u e) -> p c u e", u=2),
                in0=pairs.rearrange("p (u c e) -> p c u e", u=2, e=2),
                in1=rd_col[:].to_broadcast([P, BLOCK, 2, 2]),
                op=mybir.AluOpType.mult,
            )

        def e_quant(i):
            s = slice(i * BLOCK, (i + 1) * BLOCK)
            quant(flat(e_g[i][:]), e_c[:, s], e_s[:, s])

        def u_copy(g, b, copy):
            c = slice(b * 256, (b + 1) * 256)
            copy(
                out=u_g[g][:, c, :].rearrange("p (c i) t -> p c t i", i=4),
                in_=u_in[g][:, :, c].rearrange("p t (c i) -> p c t i", i=4),
            )

        def u_quant(g):
            s = slice(g * BANK, (g + 1) * BANK)
            quant(flat(u_g[g][:]), u_c[:, s], u_s[:, s])

        def c_mm(i, g):
            r = slice(g * BANK, (g + 1) * BANK)
            for a in range(2):
                n = slice(i * BLOCK + a * P, i * BLOCK + (a + 1) * P)
                bank = acc.tile([P, BANK], F32, name="sums")
                nc.tensor.matmul_mx(
                    out=bank[:],
                    lhsT=e_c[:, n].bitcast(FP8X4),
                    lhsT_scale=e_s[:, n],
                    rhs=u_c[:, r].bitcast(FP8X4),
                    rhs_scale=u_s[:, r],
                    start=True,
                    stop=True,
                )
                banks[("c", i, g, a)] = bank

        def wn_sub(i, g):
            for a in range(2):
                nc.vector.tensor_tensor(
                    out=wn_r[i][:, a, g, :, :, :],
                    in0=wr_in[i][:, a, g * BANK : (g + 1) * BANK].rearrange("p (k u e) -> p u k e", u=2, e=2),
                    in1=banks[("c", i, g, a)][:].rearrange("p (k u e) -> p u k e", u=2, e=2),
                    op=mybir.AluOpType.subtract,
                )

        def wn_turn(i, g):
            turn(("wn", i, g), wn_r[i], [[((a * 2 + g) * 2 + uu) * P for a in range(2)] for uu in range(2)], 1)

        def wn_unload(i, g, copy):
            b = i % 2
            unload(("wn", i, g), wn_g[i // 2][g][:, b * BLOCK : (b + 1) * BLOCK, :], copy)

        def wn_quant(h, g):
            s = slice(h * BANK, (h + 1) * BANK)
            quant(flat(wn_g[h][g][:]), wn_c[g][:, s], wn_s[g][:, s])

        def xr_turn(i, g):
            turn(("xr", i, g), xr_in[i], [[a * 512 + g * 256 + uu for a in range(2)] for uu in range(2)], 2)
            unload(("xr", i, g), xr_g[i][:, g, :, :], scopy)

        def xr_quant(i):
            quant(flat(xr_g[i][:]), flat(xr_c[i][:]), flat(xr_s[i][:]))

        def xb_turn_only(i):
            h, b = i // 2, i % 2
            turn(("xb", i), xb_in[h], [[(b * 2 + a) * 256 + uu for a in range(2)] for uu in range(2)], 2)

        def xb_unload(i):
            h, b = i // 2, i % 2
            unload(("xb", i), xb_g[h][:, b * BLOCK : (b + 1) * BLOCK, :], scopy)

        def xb_turn(i):
            xb_turn_only(i)
            xb_unload(i)

        def xb_quant(h):
            s = slice(h * 512, (h + 1) * 512)
            quant(flat(xb_g[h][:]), xb_c[:, s], xb_s[:, s])

        y32, y16, p_g, p_c = {}, {}, {}, {}

        def y_mm(h, t):
            n = slice(h * BANK, (h + 1) * BANK)
            bank = acc.tile([P, BANK], F32, name="sums")
            nc.tensor.matmul_mx(
                out=bank[:],
                lhsT=xb_c[:, t * P : (t + 1) * P].bitcast(FP8X4),
                lhsT_scale=xb_s[:, t * P : (t + 1) * P],
                rhs=q_c[:, 2 * h * BANK : 2 * (h + 1) * BANK].bitcast(FP4X4),
                rhs_scale=q_s[:, n],
                start=True,
                stop=False,
            )
            tp, b = t // 2, t % 2
            c = slice(b * P, (b + 1) * P)
            for g in range(2):
                nc.tensor.matmul_mx(
                    out=bank[:],
                    lhsT=xr_c[tp][:, g, c].bitcast(FP8X4),
                    lhsT_scale=xr_s[tp][:, g, c],
                    rhs=wn_c[g][:, n].bitcast(FP8X4),
                    rhs_scale=wn_s[g][:, n],
                    start=False,
                    stop=(g == 1),
                )
            if b == 0:
                y32_t = ring.tile([P, 2, BANK], F32, name="y32", align_bytes=64)
                y16_t = ring.tile([P, 2, 2, P, 2], BF16, name="y16", align_bytes=64, bufs=8)
                y32[(h, tp)] = y32_t
                y16[(h, tp)] = y16_t
            nc.scalar.copy(out=y32[(h, tp)][:, b, :], in_=bank[:])
            banks[("y", h, t)] = bank

        def y_round(h, t, src=None):
            tp, b = t // 2, t % 2
            src = y32[(h, tp)][:, b, :] if src is None else src
            nc.vector.tensor_copy(
                out=y16[(h, tp)][:, b, :, :, :], in_=src.rearrange("p (k u e) -> p u k e", u=2, e=2)
            )

        def y_store(h, tp):
            rows = out_0[tp * BLOCK : (tp + 1) * BLOCK, h * BANK : (h + 1) * BANK]
            nc.sync.dma_start(out=rows.rearrange("(b p) n -> p b n", p=P), in_=y32[(h, tp)][:])

        def p_turn(h, tiles):
            tp = tiles[0] // 2
            first = [[((t % 2) * 2 + uu) * P for t in tiles] for uu in range(2)]
            turn(("p", h, tiles[0]), y16[(h, tp)], first, 1)

        def p_unload(h, tiles, copy):
            w = len(tiles) * P
            p_g_t = ring.tile([P, BLOCK, 4], BF16, name="p_g", align_bytes=64)
            p_g[(h, tiles[0])] = p_g_t
            copy(
                out=flat(p_g_t[:, :w, :]).bitcast(F32).rearrange("p (c u) -> p c u", u=2),
                in_=banks[("p", h, tiles[0])][:].rearrange("p u b r -> p (b r) u"),
            )

        def p_quant(h, tiles):
            half = tiles[0] // 4
            w = len(tiles) * P
            if (h, half) not in p_c:
                p_c_t = ring.tile([P, 512], U32, name="p_c", align_bytes=64)
                p_c[(h, half)] = p_c_t
            c = tiles[0] * P - half * 512
            quant(
                flat(p_g[(h, tiles[0])][:, :w, :]),
                p_c[(h, half)][:, c : c + w],
                p_s[:, h, tiles[0] * P : tiles[0] * P + w],
            )

        def codes_store(h, t0, t1):
            half = t0 // 4
            cols = out_1[h, :, t0 * P : t1 * P, :]
            nc.sync.dma_start(
                out=cols.rearrange("p m t -> p (m t)").bitcast(I32),
                in_=p_c[(h, half)][:, (t0 - 4 * half) * P : (t1 - 4 * half) * P].bitcast(I32),
            )

        def scales_store():
            for q in range(4):
                rows = out_2.bitcast(I32)[:, 4 * q : 4 * q + 4, :]
                nc.sync.dma_start(
                    out=rows.rearrange("h r t -> r h t"),
                    in_=p_s[32 * q : 32 * q + 4, :, :].bitcast(I32),
                )

        with tc.manual_schedule():
            e_turn(0)
            e_scale(0)
            e_turn(1)
            e_scale(1)
            u_copy(0, 0, scopy)
            u_copy(0, 1, vcopy)
            e_quant(0)
            e_turn(2)
            e_scale(2)
            u_quant(0)
            e_quant(1)
            u_copy(1, 1, scopy)
            u_copy(1, 0, vcopy)
            e_turn(3)
            e_scale(3)
            u_quant(1)
            xb_turn(0)
            xb_turn(1)
            c_mm(0, 0)
            wn_sub(0, 0)
            xr_turn(0, 0)
            c_mm(0, 1)
            wn_sub(0, 1)
            xr_turn(0, 1)
            xb_turn(2)
            e_quant(2)
            c_mm(1, 1)
            wn_sub(1, 1)
            c_mm(1, 0)
            wn_sub(1, 0)
            wn_turn(0, 0)
            wn_unload(0, 0, scopy)
            wn_turn(0, 1)
            wn_unload(0, 1, scopy)
            e_quant(3)
            xr_quant(0)
            xb_turn_only(3)
            c_mm(2, 1)
            wn_sub(2, 1)
            wn_turn(1, 1)
            wn_unload(1, 1, scopy)
            xb_unload(3)
            xr_turn(1, 0)
            xr_turn(1, 1)
            xb_quant(0)
            wn_quant(0, 1)
            c_mm(2, 0)
            wn_sub(2, 0)
            xr_turn(2, 0)
            wn_turn(1, 0)
            wn_unload(1, 0, scopy)
            xr_turn(2, 1)
            wn_quant(0, 0)
            c_mm(3, 1)
            wn_sub(3, 1)
            xr_turn(3, 0)
            xr_turn(3, 1)
            c_mm(3, 0)
            wn_sub(3, 0)
            xr_quant(1)
            xr_quant(2)
            for t in range(2):
                y_mm(0, t)
            xb_quant(1)
            for i in (2, 3):
                for g in range(2):
                    wn_turn(i, g)
            wn_unload(2, 0, scopy)
            wn_unload(2, 1, scopy)
            wn_unload(3, 1, scopy)
            y_round(0, 0)
            xr_quant(3)
            wn_unload(3, 0, vcopy)
            wn_quant(1, 1)
            wn_quant(1, 0)
            y_round(0, 1)
            y_store(0, 0)
            for t in range(2, 8):
                y_mm(0, t)
                y_round(0, t)
                if t % 2 == 1:
                    y_store(0, t // 2)
            for t in range(3):
                y_mm(1, t)
            y_round(1, 0)
            y_round(1, 1)
            y_store(1, 0)
            pairs = [(2 * tp, 2 * tp + 1) for tp in range(4)]
            for tp in range(3):
                p_turn(0, pairs[tp])
            for tp in range(3):
                p_unload(0, pairs[tp], vcopy if tp == 1 else scopy)
            for tp in range(3):
                p_quant(0, pairs[tp])
            codes_store(0, 0, 4)
            y_round(1, 2)
            for t in range(3, 8):
                y_mm(1, t)
                y_round(1, t, banks[("y", 1, t)][:] if t > 5 else None)
                if t % 2 == 1:
                    y_store(1, t // 2)
            p_turn(0, pairs[3])
            p_unload(0, pairs[3], scopy)
            p_turn(1, pairs[0])
            p_unload(1, pairs[0], scopy)
            p_turn(1, pairs[1])
            p_unload(1, pairs[1], vcopy)
            p_quant(0, pairs[3])
            codes_store(0, 4, 8)
            p_turn(1, pairs[2])
            p_unload(1, pairs[2], scopy)
            p_turn(1, (6,))
            p_unload(1, (6,), scopy)
            p_quant(1, pairs[0])
            p_quant(1, pairs[1])
            codes_store(1, 0, 4)
            p_turn(1, (7,))
            p_unload(1, (7,), scopy)
            p_quant(1, pairs[2])
            p_quant(1, (6,))
            codes_store(1, 4, 7)
            p_quant(1, (7,))
            codes_store(1, 7, 8)
            scales_store()
